import numpy as np
import ml_dtypes


def mxq(x, axis, fmt="e4m3"):
    dtype, down = {"e4m3": (ml_dtypes.float8_e4m3fn, 7), "e5m2": (ml_dtypes.float8_e5m2, 14)}[fmt]
    v = np.moveaxis(np.asarray(x, np.float32).astype(ml_dtypes.bfloat16).astype(np.float64), axis, -1)
    blocks = v.reshape(v.shape[:-1] + (-1, 32))
    amax = np.abs(blocks).max(-1, keepdims=True)
    byte = np.maximum(np.where(amax > 0, np.frexp(amax)[1] - 1 + 127, 0) - down, 1)
    scale = np.exp2(byte - 127.0)
    codes = (blocks / scale).astype(np.float32).astype(dtype).astype(np.float64)
    return np.moveaxis((codes * scale).reshape(v.shape), -1, axis)


WIDE = False


def mx_kscale(k):
    if not WIDE:
        return np.ones(k)
    levels = np.array([10, -10, 5, -5, 0])
    if k % 512:
        return np.exp2(np.random.permutation(np.resize(levels, k // 32))).repeat(32)
    a = np.empty((k // 512, 16))
    for p in range(k // 512):
        a[p, :8] = np.random.permutation(np.resize(levels, 8))
        for g in range(8):
            far = levels[np.abs(levels - a[p, g]) >= 10]
            a[p, g + 8] = far[np.random.randint(len(far))]
    return np.exp2(a.ravel()).repeat(32)


def f64(x):
    return np.asarray(x).astype(np.float64)


def striped(idx):
    return np.tile(idx.reshape(-1, 16).T, (8, 1)).astype(np.uint16)


def unstriped(offs):
    return offs[:16].T.reshape(-1).astype(np.int64)


def pack_weight(w):
    k, n = w.shape
    w = f64(np.asarray(w, np.float32).astype(ml_dtypes.bfloat16)).reshape(k // 32, 32, n)
    amax = np.abs(w).max(1)
    byte = np.clip(np.where(amax > 0, np.frexp(amax)[1] - 1 + 127 - 7, 1), 1, 254)
    scaled = (w * np.exp2(127.0 - byte)[:, None, :]).reshape(k, n).astype(np.float32)
    words = np.ascontiguousarray(scaled.reshape(k // 512, 128, 4, n).transpose(0, 1, 3, 2)).astype(ml_dtypes.float8_e4m3fn).view(np.uint8)
    return words, np.ascontiguousarray(byte.astype(np.uint8).reshape(k // 512, 16, n))


def unpack_weight(words, scales):
    g, p, n, _ = words.shape
    vals = np.ascontiguousarray(words).view(ml_dtypes.float8_e4m3fn).astype(np.float64) * np.repeat(np.exp2(scales.astype(np.float64) - 127.0), 8, axis=1)[..., None]
    return vals.transpose(0, 1, 3, 2).reshape(g * 512, n)


K, T, E, C, N = 1536, 512, 8, 128, 256


def by_expert(wq, xq):
    return np.concatenate([wq[e].T @ xq[:, e * C:(e + 1) * C] for e in range(E)], axis=1)


def setup_inputs():
    n = np.random.standard_normal
    s = mx_kscale(K)[:, None]
    first = np.random.permutation(np.repeat(np.arange(E), T // E))
    second = (first + 1 + np.random.permutation(np.repeat(np.arange(E - 1), -(-T // (E - 1)))[:T])) % E
    while np.bincount(second, minlength=E).max() != T // E:
        load = np.bincount(second, minlength=E); hi, lo = int(load.argmax()), int(load.argmin())
        t = np.flatnonzero((second == hi) & (first != lo))[0]; second[t] = lo
    slot_token = np.empty(E * C, np.int64); pos = np.empty((2, T), np.int64); fill = np.zeros(E, np.int64)
    place = np.stack([np.random.permutation(C) for _ in range(E)])
    for r, deal in enumerate((first, second)):
        for t in np.random.permutation(T):
            e = deal[t]; j = e * C + place[e, fill[e]]; fill[e] += 1; slot_token[j] = t; pos[r, t] = j
    g = np.random.uniform(0.2, 0.8, T)
    packed = [pack_weight(m) for m in n((E, K, N)) / np.sqrt(K) / s[None]]
    return {
        "xT": (n((K, T)) * s).astype(np.float32),
        "w_words": np.stack([m[0] for m in packed]),
        "w_scales": np.stack([m[1] for m in packed]),
        "gate": np.stack([np.tile(g, (N, 1)), np.tile(1.0 - g, (N, 1))]).astype(np.float32),
        "offs": striped(slot_token),
        "pos1": striped(pos[0]),
        "pos2": striped(pos[1]),
    }


def reference(xT, w_words, w_scales, gate, offs, pos1, pos2):
    idx = unstriped(offs)
    xq = mxq(f64(xT)[:, idx], 0, "e4m3")
    w = np.stack([unpack_weight(w_words[e], w_scales[e]) for e in range(E)])
    y = by_expert(w, xq)
    return f64(gate[0]) * y[:, unstriped(pos1)] + f64(gate[1]) * y[:, unstriped(pos2)]

@@ -1,0 +1,144 @@
+from contextlib import ExitStack
+
+import concourse.mybir as mybir
+
+K, T, E, C, N = 1536, 512, 8, 128, 256
+FLOPS = 2 * E * C * K * N
+
+F32 = mybir.dt.float32
+BF16 = mybir.dt.bfloat16
+I32 = mybir.dt.int32
+U32 = mybir.dt.uint32
+U16 = mybir.dt.uint16
+U8 = mybir.dt.uint8
+FP8X4 = mybir.dt.float8_e4m3fn_x4
+MULT = mybir.AluOpType.mult
+
+P = 128
+PASSES = K // 512
+BLOCKS = N // P
+
+CHUNKS = [(0, 3), (3, 5), (5, 7), (7, 8)]
+CUTS = [(0, 3), (3, 6), (6, 8)]
+WLOADS = [(e, e + 1) for e in (0, 3, 5, 7, 1, 2, 4, 6)]
+PIECES = [
+    [(0, 256, 80), (256, 256, 80)],
+    [(0, 512, 320)],
+    [(0, 512, 512)],
+]
+
+
+def tile_routed_moe_kernel(tc, xT, w_words, w_scales, gate, offs, pos1, pos2, out):
+    nc = tc.nc
+    with ExitStack() as ctx:
+        held = ctx.enter_context(tc.tile_pool(name="held", bufs=1))
+        psum = ctx.enter_context(tc.psum_pool(name="psum", bufs=1))
+
+        offs_t = held.tile([P, E * C // 16], U16, name="offs_t")
+        pos_t = [held.tile([P, T // 16], U16, name=f"pos{r}_t") for r in range(2)]
+
+        xv = xT.rearrange("(g p t) n -> g p t n", p=P, t=4)
+        raw = {}
+        for g in range(PASSES):
+            for c0, width, _ in PIECES[g]:
+                raw[g, c0] = held.tile([P, 4, width], F32, name=f"raw{g}_{c0}")
+                nc.sync.dma_start(out=raw[g, c0][:], in_=xv[g, :, :, c0 : c0 + width])
+            if g == 0:
+                nc.sync.dma_start(offs_t[:], offs)
+
+        planes = held.tile([P, T], U8, align_bytes=64, name="planes")
+        nc.gpsimd.memset(planes[:], 0)
+        w_sc = held.tile([P, E * PASSES, N], U8, align_bytes=64, name="w_sc")
+        nc.vector.memset(w_sc[:].bitcast(I32), 0)
+        scv = w_scales.rearrange("e a (q i) n -> q i (e a) n", i=4)
+        for q in range(4):
+            nc.sync.dma_start(out=w_sc[32 * q : 32 * q + 4, :, :].bitcast(I32), in_=scv[q].bitcast(I32))
+
+        w_t = {}
+        for e0, e1 in WLOADS:
+            wt = held.tile([P, (e1 - e0) * PASSES, N], U32, align_bytes=64, name=f"w{e0}")
+            nc.sync.dma_start(out=wt[:].bitcast(I32), in_=w_words[e0:e1].rearrange("e a p n r -> p (e a) (n r)").bitcast(I32))
+            for e in range(e0, e1):
+                for a in range(PASSES):
+                    w_t[e, a] = wt[:, (e - e0) * PASSES + a, :]
+
+        nc.sync.dma_start(pos_t[0][:], pos1)
+        nc.sync.dma_start(pos_t[1][:], pos2)
+        gv = gate.rearrange("r (m p) t -> m p r t", p=P)
+        gate_t = []
+        for m in range(BLOCKS):
+            gt = held.tile([P, 2, T], F32, name=f"gate{m}")
+            nc.sync.dma_start(out=gt[:], in_=gv[m])
+            gate_t.append(gt)
+
+        words = [held.tile([P, T], U32, align_bytes=64, name=f"words{g}") for g in range(PASSES)]
+        g_words = held.tile([P, PASSES, E * C], U32, align_bytes=64, name="g_words")
+        g_planes = held.tile([P, E * C], U8, align_bytes=64, name="g_planes")
+
+        def interleave(dst, src):
+            return dst.rearrange("p (c i) t -> p c t i", i=4), src.rearrange("p t (c i) -> p c t i", i=4)
+
+        def quantise(g):
+            for c0, width, cs in PIECES[g]:
+                src = raw[g, c0]
+                bf = held.tile([P, width, 4], BF16, align_bytes=64, name=f"bf{g}_{c0}")
+                o, i = interleave(bf[:, :cs, :], src[:, :, :cs])
+                nc.scalar.copy(o, i)
+                if cs < width:
+                    o, i = interleave(bf[:, cs:, :], src[:, :, cs:])
+                    nc.vector.tensor_copy(o, i)
+                nc.vector.quantize_mx(
+                    out=words[g][:, c0 : c0 + width].bitcast(FP8X4),
+                    scales=planes[4 * g : P, c0 : c0 + width],
+                    in_=bf[:].rearrange("p n t -> p (n t)"),
+                )
+
+        def gather(dst, src, e0, e1):
+            nc.vector.tensor_copy(dst, src[:].indirect(offs_t[:, e0 * C // 16 : e1 * C // 16]))
+
+        for g in range(PASSES - 1):
+            quantise(g)
+            for e0, e1 in CUTS:
+                gather(g_words[:, g, e0 * C : e1 * C], words[g], e0, e1)
+        quantise(PASSES - 1)
+
+        for e0, e1 in CUTS:
+            gather(g_planes[:, e0 * C : e1 * C], planes, e0, e1)
+
+        y = [held.tile([P, E * C], F32, name=f"y{m}") for m in range(BLOCKS)]
+        acc = {}
+        for e0, e1 in CHUNKS:
+            for m in range(BLOCKS):
+                acc[e0, m] = psum.tile([P, (e1 - e0) * C], F32, name=f"acc{m}_{e0}")
+
+        def multiply(e0, e, m, a):
+            nc.tensor.matmul_mx(
+                out=acc[e0, m][:, (e - e0) * C : (e - e0 + 1) * C],
+                lhsT=w_t[e, a][:, m * P : (m + 1) * P].bitcast(FP8X4),
+                lhsT_scale=w_sc[:, e * PASSES + a, m * P : (m + 1) * P],
+                rhs=g_words[:, a, e * C : (e + 1) * C].bitcast(FP8X4),
+                rhs_scale=g_planes[4 * a : P, e * C : (e + 1) * C],
+                start=(a == 0),
+                stop=(a == PASSES - 1),
+            )
+
+        for e0, e1 in CHUNKS:
+            for m in range(BLOCKS):
+                for a in range(PASSES - 1):
+                    multiply(e0, e0, m, a)
+        for e0, e1 in CHUNKS:
+            gather(g_words[:, PASSES - 1, e0 * C : e1 * C], words[PASSES - 1], e0, e1)
+            for m in range(BLOCKS):
+                multiply(e0, e0, m, PASSES - 1)
+                for e in range(e0 + 1, e1):
+                    for a in range(PASSES):
+                        multiply(e0, e, m, a)
+                nc.scalar.copy(y[m][:, e0 * C : e1 * C], acc[e0, m][:])
+
+        for m in range(BLOCKS):
+            prod = [held.tile([P, T], F32, name=f"prod{m}_{r}") for r in range(2)]
+            for r in range(2):
+                nc.vector.tensor_tensor(prod[r][:], y[m][:].indirect(pos_t[r][:]), gate_t[m][:, r, :], MULT)
+            total = held.tile([P, T], F32, name=f"total{m}")
+            nc.vector.tensor_add(total[:], prod[0][:], prod[1][:])
+            nc.sync.dma_start(out=out[m * P : (m + 1) * P, :], in_=total[:])

@@ -18,14 +18,11 @@ P = 128
 PASSES = K // 512
 BLOCKS = N // P
 
-CHUNKS = [(0, 3), (3, 5), (5, 7), (7, 8)]
 CUTS = [(0, 3), (3, 6), (6, 8)]
-WLOADS = [(e, e + 1) for e in (0, 3, 5, 7, 1, 2, 4, 6)]
-PIECES = [
-    [(0, 256, 80), (256, 256, 80)],
-    [(0, 512, 320)],
-    [(0, 512, 512)],
-]
+LAST_CUTS = {0: [(0, 3)], 3: [(3, 6)], 6: [(6, 7), (7, 8)]}
+WHOLE = [(0, 2), (2, 4), (4, 5)]
+HALVES = [[(5, 7), (7, 8)], [(5, 8)]]
+SCALAR_CASTS = [192, 512, 512]
 
 
 def tile_routed_moe_kernel(tc, xT, w_words, w_scales, gate, offs, pos1, pos2, out):
@@ -38,38 +35,48 @@ def tile_routed_moe_kernel(tc, xT, w_words, w_scales, gate, offs, pos1, pos2, ou
         pos_t = [held.tile([P, T // 16], U16, name=f"pos{r}_t") for r in range(2)]
 
         xv = xT.rearrange("(g p t) n -> g p t n", p=P, t=4)
-        raw = {}
-        for g in range(PASSES):
-            for c0, width, _ in PIECES[g]:
-                raw[g, c0] = held.tile([P, 4, width], F32, name=f"raw{g}_{c0}")
-                nc.sync.dma_start(out=raw[g, c0][:], in_=xv[g, :, :, c0 : c0 + width])
-            if g == 0:
-                nc.sync.dma_start(offs_t[:], offs)
+        raw = [held.tile([P, 4, T], F32, name=f"raw{g}") for g in range(PASSES)]
+        nc.sync.dma_start(out=raw[0][:], in_=xv[0])
+        nc.sync.dma_start(offs_t[:], offs)
+        for g in range(1, PASSES):
+            nc.sync.dma_start(out=raw[g][:], in_=xv[g])
 
         planes = held.tile([P, T], U8, align_bytes=64, name="planes")
         nc.gpsimd.memset(planes[:], 0)
         w_sc = held.tile([P, E * PASSES, N], U8, align_bytes=64, name="w_sc")
-        nc.vector.memset(w_sc[:].bitcast(I32), 0)
+        nc.gpsimd.memset(w_sc[:].bitcast(I32), 0)
         scv = w_scales.rearrange("e a (q i) n -> q i (e a) n", i=4)
         for q in range(4):
             nc.sync.dma_start(out=w_sc[32 * q : 32 * q + 4, :, :].bitcast(I32), in_=scv[q].bitcast(I32))
 
         w_t = {}
-        for e0, e1 in WLOADS:
-            wt = held.tile([P, (e1 - e0) * PASSES, N], U32, align_bytes=64, name=f"w{e0}")
-            nc.sync.dma_start(out=wt[:].bitcast(I32), in_=w_words[e0:e1].rearrange("e a p n r -> p (e a) (n r)").bitcast(I32))
+
+        def load_weights(e0, e1, m0, m1):
+            wt = held.tile([P, (e1 - e0) * PASSES, (m1 - m0) * P], U32, align_bytes=64, name=f"w{e0}_{m0}")
+            src = w_words[e0:e1, :, :, m0 * P : m1 * P, :].rearrange("e a p n r -> p (e a) (n r)")
+            nc.sync.dma_start(out=wt[:].bitcast(I32), in_=src.bitcast(I32))
             for e in range(e0, e1):
                 for a in range(PASSES):
-                    w_t[e, a] = wt[:, (e - e0) * PASSES + a, :]
+                    for m in range(m0, m1):
+                        w_t[e, a, m] = wt[:, (e - e0) * PASSES + a, (m - m0) * P : (m - m0 + 1) * P]
 
+        gate_t = {}
+
+        def load_gate(m):
+            for r in range(2):
+                gate_t[m, r] = held.tile([P, T], F32, name=f"gate{m}_{r}")
+                nc.sync.dma_start(out=gate_t[m, r][:], in_=gate[r, m * P : (m + 1) * P, :])
+
+        for e0, e1 in WHOLE:
+            load_weights(e0, e1, 0, BLOCKS)
         nc.sync.dma_start(pos_t[0][:], pos1)
+        for e0, e1 in HALVES[0]:
+            load_weights(e0, e1, 0, 1)
         nc.sync.dma_start(pos_t[1][:], pos2)
-        gv = gate.rearrange("r (m p) t -> m p r t", p=P)
-        gate_t = []
-        for m in range(BLOCKS):
-            gt = held.tile([P, 2, T], F32, name=f"gate{m}")
-            nc.sync.dma_start(out=gt[:], in_=gv[m])
-            gate_t.append(gt)
+        load_gate(0)
+        for e0, e1 in HALVES[1]:
+            load_weights(e0, e1, 1, 2)
+        load_gate(1)
 
         words = [held.tile([P, T], U32, align_bytes=64, name=f"words{g}") for g in range(PASSES)]
         g_words = held.tile([P, PASSES, E * C], U32, align_bytes=64, name="g_words")
@@ -79,19 +86,18 @@ def tile_routed_moe_kernel(tc, xT, w_words, w_scales, gate, offs, pos1, pos2, ou
             return dst.rearrange("p (c i) t -> p c t i", i=4), src.rearrange("p t (c i) -> p c t i", i=4)
 
         def quantise(g):
-            for c0, width, cs in PIECES[g]:
-                src = raw[g, c0]
-                bf = held.tile([P, width, 4], BF16, align_bytes=64, name=f"bf{g}_{c0}")
-                o, i = interleave(bf[:, :cs, :], src[:, :, :cs])
-                nc.scalar.copy(o, i)
-                if cs < width:
-                    o, i = interleave(bf[:, cs:, :], src[:, :, cs:])
-                    nc.vector.tensor_copy(o, i)
-                nc.vector.quantize_mx(
-                    out=words[g][:, c0 : c0 + width].bitcast(FP8X4),
-                    scales=planes[4 * g : P, c0 : c0 + width],
-                    in_=bf[:].rearrange("p n t -> p (n t)"),
-                )
+            cs = SCALAR_CASTS[g]
+            bf = held.tile([P, T, 4], BF16, align_bytes=64, name=f"bf{g}")
+            o, i = interleave(bf[:, :cs, :], raw[g][:, :, :cs])
+            nc.scalar.copy(o, i)
+            if cs < T:
+                o, i = interleave(bf[:, cs:, :], raw[g][:, :, cs:])
+                nc.vector.tensor_copy(o, i)
+            nc.vector.quantize_mx(
+                out=words[g][:].bitcast(FP8X4),
+                scales=planes[4 * g : P, :],
+                in_=bf[:].rearrange("p n t -> p (n t)"),
+            )
 
         def gather(dst, src, e0, e1):
             nc.vector.tensor_copy(dst, src[:].indirect(offs_t[:, e0 * C // 16 : e1 * C // 16]))
@@ -102,43 +108,35 @@ def tile_routed_moe_kernel(tc, xT, w_words, w_scales, gate, offs, pos1, pos2, ou
                 gather(g_words[:, g, e0 * C : e1 * C], words[g], e0, e1)
         quantise(PASSES - 1)
 
-        for e0, e1 in CUTS:
-            gather(g_planes[:, e0 * C : e1 * C], planes, e0, e1)
-
         y = [held.tile([P, E * C], F32, name=f"y{m}") for m in range(BLOCKS)]
-        acc = {}
-        for e0, e1 in CHUNKS:
-            for m in range(BLOCKS):
-                acc[e0, m] = psum.tile([P, (e1 - e0) * C], F32, name=f"acc{m}_{e0}")
 
-        def multiply(e0, e, m, a):
-            nc.tensor.matmul_mx(
-                out=acc[e0, m][:, (e - e0) * C : (e - e0 + 1) * C],
-                lhsT=w_t[e, a][:, m * P : (m + 1) * P].bitcast(FP8X4),
-                lhsT_scale=w_sc[:, e * PASSES + a, m * P : (m + 1) * P],
-                rhs=g_words[:, a, e * C : (e + 1) * C].bitcast(FP8X4),
-                rhs_scale=g_planes[4 * a : P, e * C : (e + 1) * C],
-                start=(a == 0),
-                stop=(a == PASSES - 1),
-            )
+        def multiply(m, e0, e1):
+            acc = psum.tile([P, (e1 - e0) * C], F32, name=f"acc{m}_{e0}")
+            for e in range(e0, e1):
+                for a in range(PASSES):
+                    nc.tensor.matmul_mx(
+                        out=acc[:, (e - e0) * C : (e - e0 + 1) * C],
+                        lhsT=w_t[e, a, m].bitcast(FP8X4),
+                        lhsT_scale=w_sc[:, e * PASSES + a, m * P : (m + 1) * P],
+                        rhs=g_words[:, a, e * C : (e + 1) * C].bitcast(FP8X4),
+                        rhs_scale=g_planes[4 * a : P, e * C : (e + 1) * C],
+                        start=(a == 0),
+                        stop=(a == PASSES - 1),
+                    )
+            nc.scalar.copy(y[m][:, e0 * C : e1 * C], acc[:])
 
-        for e0, e1 in CHUNKS:
-            for m in range(BLOCKS):
-                for a in range(PASSES - 1):
-                    multiply(e0, e0, m, a)
-        for e0, e1 in CHUNKS:
-            gather(g_words[:, PASSES - 1, e0 * C : e1 * C], words[PASSES - 1], e0, e1)
-            for m in range(BLOCKS):
-                multiply(e0, e0, m, PASSES - 1)
-                for e in range(e0 + 1, e1):
-                    for a in range(PASSES):
-                        multiply(e0, e, m, a)
-                nc.scalar.copy(y[m][:, e0 * C : e1 * C], acc[e0, m][:])
+        for c0, c1 in CUTS:
+            gather(g_planes[:, c0 * C : c1 * C], planes, c0, c1)
+            for e0, e1 in LAST_CUTS[c0]:
+                gather(g_words[:, PASSES - 1, e0 * C : e1 * C], words[PASSES - 1], e0, e1)
+                multiply(0, e0, e1)
+        for e0, e1 in [(0, 3), (3, 6), (6, 8)]:
+            multiply(1, e0, e1)
 
         for m in range(BLOCKS):
             prod = [held.tile([P, T], F32, name=f"prod{m}_{r}") for r in range(2)]
             for r in range(2):
-                nc.vector.tensor_tensor(prod[r][:], y[m][:].indirect(pos_t[r][:]), gate_t[m][:, r, :], MULT)
+                nc.vector.tensor_tensor(prod[r][:], y[m][:].indirect(pos_t[r][:]), gate_t[m, r][:], MULT)
             total = held.tile([P, T], F32, name=f"total{m}")
             nc.vector.tensor_add(total[:], prod[0][:], prod[1][:])
             nc.sync.dma_start(out=out[m * P : (m + 1) * P, :], in_=total[:])

@@ -1,6 +1,7 @@
 from contextlib import ExitStack
 
 import concourse.mybir as mybir
+from concourse.masks import make_identity
 
 K, T, E, C, N = 1536, 512, 8, 128, 256
 FLOPS = 2 * E * C * K * N
@@ -16,13 +17,17 @@ MULT = mybir.AluOpType.mult
 
 P = 128
 PASSES = K // 512
+LAST = PASSES - 1
 BLOCKS = N // P
 
-CUTS = [(0, 3), (3, 6), (6, 8)]
-LAST_CUTS = {0: [(0, 3)], 3: [(3, 6)], 6: [(6, 7), (7, 8)]}
 WHOLE = [(0, 2), (2, 4), (4, 5)]
 HALVES = [[(5, 7), (7, 8)], [(5, 8)]]
-SCALAR_CASTS = [192, 512, 512]
+PIECES = [
+    [(0, 2, 176, 0, 336), (2, 2, 176, 0, 336)],
+    [(0, 4, 416, 96, 0)],
+    [(0, 4, 512, 0, 0)],
+]
+WINDOW = 1536
 
 
 def tile_routed_moe_kernel(tc, xT, w_words, w_scales, gate, offs, pos1, pos2, out):
@@ -35,19 +40,25 @@ def tile_routed_moe_kernel(tc, xT, w_words, w_scales, gate, offs, pos1, pos2, ou
         pos_t = [held.tile([P, T // 16], U16, name=f"pos{r}_t") for r in range(2)]
 
         xv = xT.rearrange("(g p t) n -> g p t n", p=P, t=4)
-        raw = [held.tile([P, 4, T], F32, name=f"raw{g}") for g in range(PASSES)]
-        nc.sync.dma_start(out=raw[0][:], in_=xv[0])
-        nc.sync.dma_start(offs_t[:], offs)
-        for g in range(1, PASSES):
-            nc.sync.dma_start(out=raw[g][:], in_=xv[g])
+        raw = {}
+        for g in range(PASSES):
+            for t, nt, _, _, _ in PIECES[g]:
+                raw[g, t] = held.tile([P, nt, T], F32, name=f"raw{g}_{t}")
+                nc.sync.dma_start(out=raw[g, t][:], in_=xv[g, :, t : t + nt, :])
+            if g == 0:
+                nc.sync.dma_start(offs_t[:], offs)
 
-        planes = held.tile([P, T], U8, align_bytes=64, name="planes")
+        planes = held.tile([P, WINDOW], U8, align_bytes=64, name="planes")
         nc.gpsimd.memset(planes[:], 0)
+        words = held.tile([P, 2 * T + WINDOW], I32, align_bytes=64, name="words")
+        nc.vector.memset(words[:, PASSES * T :], 0)
         w_sc = held.tile([P, E * PASSES, N], U8, align_bytes=64, name="w_sc")
         nc.gpsimd.memset(w_sc[:].bitcast(I32), 0)
-        scv = w_scales.rearrange("e a (q i) n -> q i (e a) n", i=4)
-        for q in range(4):
-            nc.sync.dma_start(out=w_sc[32 * q : 32 * q + 4, :, :].bitcast(I32), in_=scv[q].bitcast(I32))
+        ident = held.tile([P, P], F32, name="ident")
+        make_identity(nc, ident[:])
+        scv = w_scales.rearrange("e a (q i) n -> i q (e a) n", i=4)
+        for i in range(4):
+            nc.sync.dma_start(out=w_sc[i:P:32, :, :].bitcast(I32), in_=scv[i].bitcast(I32))
 
         w_t = {}
 
@@ -78,7 +89,6 @@ def tile_routed_moe_kernel(tc, xT, w_words, w_scales, gate, offs, pos1, pos2, ou
             load_weights(e0, e1, 1, 2)
         load_gate(1)
 
-        words = [held.tile([P, T], U32, align_bytes=64, name=f"words{g}") for g in range(PASSES)]
         g_words = held.tile([P, PASSES, E * C], U32, align_bytes=64, name="g_words")
         g_planes = held.tile([P, E * C], U8, align_bytes=64, name="g_planes")
 
@@ -86,57 +96,86 @@ def tile_routed_moe_kernel(tc, xT, w_words, w_scales, gate, offs, pos1, pos2, ou
             return dst.rearrange("p (c i) t -> p c t i", i=4), src.rearrange("p t (c i) -> p c t i", i=4)
 
         def quantise(g):
-            cs = SCALAR_CASTS[g]
             bf = held.tile([P, T, 4], BF16, align_bytes=64, name=f"bf{g}")
-            o, i = interleave(bf[:, :cs, :], raw[g][:, :, :cs])
-            nc.scalar.copy(o, i)
-            if cs < T:
-                o, i = interleave(bf[:, cs:, :], raw[g][:, :, cs:])
-                nc.vector.tensor_copy(o, i)
+            for t, nt, *shares in PIECES[g]:
+                n = 0
+                for copy, width in zip((nc.scalar.copy, nc.gpsimd.tensor_copy, nc.vector.tensor_copy), shares):
+                    if width:
+                        copy(*interleave(bf[:, n : n + width, t : t + nt], raw[g, t][:, :, n : n + width]))
+                    n += width
+            first = (LAST - g) * T
             nc.vector.quantize_mx(
-                out=words[g][:].bitcast(FP8X4),
-                scales=planes[4 * g : P, :],
+                out=words[:, first : first + T].bitcast(FP8X4),
+                scales=planes[4 * g : P, :T],
                 in_=bf[:].rearrange("p n t -> p (n t)"),
             )
+            return words[:, first : first + WINDOW].bitcast(U32)
 
-        def gather(dst, src, e0, e1):
-            nc.vector.tensor_copy(dst, src[:].indirect(offs_t[:, e0 * C // 16 : e1 * C // 16]))
+        def gather(dst, window, e0, e1):
+            nc.vector.tensor_copy(dst, window.indirect(offs_t[:, e0 * C // 16 : e1 * C // 16]))
 
-        for g in range(PASSES - 1):
-            quantise(g)
-            for e0, e1 in CUTS:
-                gather(g_words[:, g, e0 * C : e1 * C], words[g], e0, e1)
-        quantise(PASSES - 1)
+        for g in range(LAST):
+            gather(g_words[:, g, :], quantise(g), 0, E)
+        last_words = quantise(LAST)[:, :T]
+        gather(g_planes[:], planes[:], 0, E)
 
         y = [held.tile([P, E * C], F32, name=f"y{m}") for m in range(BLOCKS)]
 
-        def multiply(m, e0, e1):
-            acc = psum.tile([P, (e1 - e0) * C], F32, name=f"acc{m}_{e0}")
-            for e in range(e0, e1):
-                for a in range(PASSES):
-                    nc.tensor.matmul_mx(
-                        out=acc[:, (e - e0) * C : (e - e0 + 1) * C],
-                        lhsT=w_t[e, a, m].bitcast(FP8X4),
-                        lhsT_scale=w_sc[:, e * PASSES + a, m * P : (m + 1) * P],
-                        rhs=g_words[:, a, e * C : (e + 1) * C].bitcast(FP8X4),
-                        rhs_scale=g_planes[4 * a : P, e * C : (e + 1) * C],
-                        start=(a == 0),
-                        stop=(a == PASSES - 1),
-                    )
-            nc.scalar.copy(y[m][:, e0 * C : e1 * C], acc[:])
+        acc = {}
 
-        for c0, c1 in CUTS:
-            gather(g_planes[:, c0 * C : c1 * C], planes, c0, c1)
-            for e0, e1 in LAST_CUTS[c0]:
-                gather(g_words[:, PASSES - 1, e0 * C : e1 * C], words[PASSES - 1], e0, e1)
-                multiply(0, e0, e1)
-        for e0, e1 in [(0, 3), (3, 6), (6, 8)]:
-            multiply(1, e0, e1)
+        def accumulator(m, e0, e1, tag):
+            tile = psum.tile([P, (e1 - e0) * C], F32, name=f"acc{m}_{e0}", tag=tag)
+            for e in range(e0, e1):
+                acc[m, e] = tile[:, (e - e0) * C : (e - e0 + 1) * C]
+            return tile
+
+        def multiply(m, e, passes):
+            for a in passes:
+                nc.tensor.matmul_mx(
+                    out=acc[m, e],
+                    lhsT=w_t[e, a, m].bitcast(FP8X4),
+                    lhsT_scale=w_sc[:, e * PASSES + a, m * P : (m + 1) * P],
+                    rhs=g_words[:, a, e * C : (e + 1) * C].bitcast(FP8X4),
+                    rhs_scale=g_planes[4 * a : P, e * C : (e + 1) * C],
+                    start=(a == 0),
+                    stop=(a == LAST),
+                )
+
+        bank = 0
+        for e0, e1 in ((0, 3), (3, 6), (6, 7), (7, 8)):
+            groups = [(e, e + 1) for e in range(e0, e1)] if e0 != 3 else [(e0, e1)]
+            tiles = []
+            for f0, f1 in groups:
+                tiles.append(accumulator(0, f0, f1, f"bank{bank}"))
+                bank += 1
+                multiply(0, f0, range(LAST))
+            gather(g_words[:, LAST, e0 * C : e1 * C], last_words, e0, e1)
+            for (f0, f1), tile in zip(groups, tiles):
+                multiply(0, f0, [LAST])
+                for e in range(f0 + 1, f1):
+                    multiply(0, e, range(PASSES))
+                copy = nc.vector.tensor_copy if f1 == E else nc.scalar.copy
+                copy(y[0][:, f0 * C : f1 * C], tile[:])
+        for (e0, e1), tag in zip(((0, 3), (3, 6), (6, 8)), ("bank4", "bank5", "bank4")):
+            tile = accumulator(1, e0, e1, tag)
+            for e in range(e0, e1):
+                multiply(1, e, range(PASSES))
+            nc.scalar.copy(y[1][:, e0 * C : e1 * C], tile[:])
+
+        prod = {}
+        total = [held.tile([P, T], F32, name=f"total{m}") for m in range(BLOCKS)]
+
+        def pick(m, r):
+            prod[m, r] = held.tile([P, T], F32, name=f"prod{m}_{r}")
+            nc.vector.tensor_tensor(prod[m, r][:], y[m][:].indirect(pos_t[r][:]), gate_t[m, r][:], MULT)
 
         for m in range(BLOCKS):
-            prod = [held.tile([P, T], F32, name=f"prod{m}_{r}") for r in range(2)]
             for r in range(2):
-                nc.vector.tensor_tensor(prod[r][:], y[m][:].indirect(pos_t[r][:]), gate_t[m, r][:], MULT)
-            total = held.tile([P, T], F32, name=f"total{m}")
-            nc.vector.tensor_add(total[:], prod[0][:], prod[1][:])
-            nc.sync.dma_start(out=out[m * P : (m + 1) * P, :], in_=total[:])
+                pick(m, r)
+        both = psum.tile([P, T], F32, name="both", tag="bank5")
+        for r in range(2):
+            nc.tensor.matmul(both[:], ident[:], prod[0, r][:], start=(r == 0), stop=(r == 1))
+        nc.scalar.copy(total[0][:], both[:])
+        nc.vector.tensor_add(total[1][:], prod[1, 0][:], prod[1, 1][:])
+        for m in range(BLOCKS):
+            nc.sync.dma_start(out=out[m * P : (m + 1) * P, :], in_=total[m][:])

from contextlib import ExitStack

import concourse.mybir as mybir
from concourse.masks import make_identity

K, T, E, C, N = 1536, 512, 8, 128, 256
FLOPS = 2 * E * C * K * N

F32 = mybir.dt.float32
BF16 = mybir.dt.bfloat16
I32 = mybir.dt.int32
U32 = mybir.dt.uint32
U16 = mybir.dt.uint16
U8 = mybir.dt.uint8
FP8X4 = mybir.dt.float8_e4m3fn_x4
MULT = mybir.AluOpType.mult

P = 128
PASSES = K // 512
LAST = PASSES - 1
BLOCKS = N // P

WHOLE = [(0, 2), (2, 4), (4, 5)]
HALVES = [[(5, 7), (7, 8)], [(5, 8)]]
PIECES = [
    [(0, 2, 176, 0, 336), (2, 2, 176, 0, 336)],
    [(0, 4, 416, 96, 0)],
    [(0, 4, 512, 0, 0)],
]
WINDOW = 1536


def tile_routed_moe_kernel(tc, xT, w_words, w_scales, gate, offs, pos1, pos2, out):
    nc = tc.nc
    with ExitStack() as ctx:
        held = ctx.enter_context(tc.tile_pool(name="held", bufs=1))
        psum = ctx.enter_context(tc.psum_pool(name="psum", bufs=1))

        offs_t = held.tile([P, E * C // 16], U16, name="offs_t")
        pos_t = [held.tile([P, T // 16], U16, name=f"pos{r}_t") for r in range(2)]

        xv = xT.rearrange("(g p t) n -> g p t n", p=P, t=4)
        raw = {}
        for g in range(PASSES):
            for t, nt, _, _, _ in PIECES[g]:
                raw[g, t] = held.tile([P, nt, T], F32, name=f"raw{g}_{t}")
                nc.sync.dma_start(out=raw[g, t][:], in_=xv[g, :, t : t + nt, :])
            if g == 0:
                nc.sync.dma_start(offs_t[:], offs)

        planes = held.tile([P, WINDOW], U8, align_bytes=64, name="planes")
        nc.gpsimd.memset(planes[:], 0)
        words = held.tile([P, 2 * T + WINDOW], I32, align_bytes=64, name="words")
        nc.vector.memset(words[:, PASSES * T :], 0)
        w_sc = held.tile([P, E * PASSES, N], U8, align_bytes=64, name="w_sc")
        nc.gpsimd.memset(w_sc[:].bitcast(I32), 0)
        ident = held.tile([P, P], F32, name="ident")
        make_identity(nc, ident[:])
        scv = w_scales.rearrange("e a (q i) n -> i q (e a) n", i=4)
        for i in range(4):
            nc.sync.dma_start(out=w_sc[i:P:32, :, :].bitcast(I32), in_=scv[i].bitcast(I32))

        w_t = {}

        def load_weights(e0, e1, m0, m1):
            wt = held.tile([P, (e1 - e0) * PASSES, (m1 - m0) * P], U32, align_bytes=64, name=f"w{e0}_{m0}")
            src = w_words[e0:e1, :, :, m0 * P : m1 * P, :].rearrange("e a p n r -> p (e a) (n r)")
            nc.sync.dma_start(out=wt[:].bitcast(I32), in_=src.bitcast(I32))
            for e in range(e0, e1):
                for a in range(PASSES):
                    for m in range(m0, m1):
                        w_t[e, a, m] = wt[:, (e - e0) * PASSES + a, (m - m0) * P : (m - m0 + 1) * P]

        gate_t = {}

        def load_gate(m):
            for r in range(2):
                gate_t[m, r] = held.tile([P, T], F32, name=f"gate{m}_{r}")
                nc.sync.dma_start(out=gate_t[m, r][:], in_=gate[r, m * P : (m + 1) * P, :])

        for e0, e1 in WHOLE:
            load_weights(e0, e1, 0, BLOCKS)
        nc.sync.dma_start(pos_t[0][:], pos1)
        for e0, e1 in HALVES[0]:
            load_weights(e0, e1, 0, 1)
        nc.sync.dma_start(pos_t[1][:], pos2)
        load_gate(0)
        for e0, e1 in HALVES[1]:
            load_weights(e0, e1, 1, 2)
        load_gate(1)

        g_words = held.tile([P, PASSES, E * C], U32, align_bytes=64, name="g_words")
        g_planes = held.tile([P, E * C], U8, align_bytes=64, name="g_planes")

        def interleave(dst, src):
            return dst.rearrange("p (c i) t -> p c t i", i=4), src.rearrange("p t (c i) -> p c t i", i=4)

        def quantise(g):
            bf = held.tile([P, T, 4], BF16, align_bytes=64, name=f"bf{g}")
            for t, nt, *shares in PIECES[g]:
                n = 0
                for copy, width in zip((nc.scalar.copy, nc.gpsimd.tensor_copy, nc.vector.tensor_copy), shares):
                    if width:
                        copy(*interleave(bf[:, n : n + width, t : t + nt], raw[g, t][:, :, n : n + width]))
                    n += width
            first = (LAST - g) * T
            nc.vector.quantize_mx(
                out=words[:, first : first + T].bitcast(FP8X4),
                scales=planes[4 * g : P, :T],
                in_=bf[:].rearrange("p n t -> p (n t)"),
            )
            return words[:, first : first + WINDOW].bitcast(U32)

        def gather(dst, window, e0, e1):
            nc.vector.tensor_copy(dst, window.indirect(offs_t[:, e0 * C // 16 : e1 * C // 16]))

        for g in range(LAST):
            gather(g_words[:, g, :], quantise(g), 0, E)
        last_words = quantise(LAST)[:, :T]
        gather(g_planes[:], planes[:], 0, E)

        y = [held.tile([P, E * C], F32, name=f"y{m}") for m in range(BLOCKS)]

        acc = {}

        def accumulator(m, e0, e1, tag):
            tile = psum.tile([P, (e1 - e0) * C], F32, name=f"acc{m}_{e0}", tag=tag)
            for e in range(e0, e1):
                acc[m, e] = tile[:, (e - e0) * C : (e - e0 + 1) * C]
            return tile

        def multiply(m, e, passes):
            for a in passes:
                nc.tensor.matmul_mx(
                    out=acc[m, e],
                    lhsT=w_t[e, a, m].bitcast(FP8X4),
                    lhsT_scale=w_sc[:, e * PASSES + a, m * P : (m + 1) * P],
                    rhs=g_words[:, a, e * C : (e + 1) * C].bitcast(FP8X4),
                    rhs_scale=g_planes[4 * a : P, e * C : (e + 1) * C],
                    start=(a == 0),
                    stop=(a == LAST),
                )

        bank = 0
        for e0, e1 in ((0, 3), (3, 6), (6, 7), (7, 8)):
            groups = [(e, e + 1) for e in range(e0, e1)] if e0 != 3 else [(e0, e1)]
            tiles = []
            for f0, f1 in groups:
                tiles.append(accumulator(0, f0, f1, f"bank{bank}"))
                bank += 1
                multiply(0, f0, range(LAST))
            gather(g_words[:, LAST, e0 * C : e1 * C], last_words, e0, e1)
            for (f0, f1), tile in zip(groups, tiles):
                multiply(0, f0, [LAST])
                for e in range(f0 + 1, f1):
                    multiply(0, e, range(PASSES))
                copy = nc.vector.tensor_copy if f1 == E else nc.scalar.copy
                copy(y[0][:, f0 * C : f1 * C], tile[:])
        for (e0, e1), tag in zip(((0, 3), (3, 6), (6, 8)), ("bank4", "bank5", "bank4")):
            tile = accumulator(1, e0, e1, tag)
            for e in range(e0, e1):
                multiply(1, e, range(PASSES))
            nc.scalar.copy(y[1][:, e0 * C : e1 * C], tile[:])

        prod = {}
        total = [held.tile([P, T], F32, name=f"total{m}") for m in range(BLOCKS)]

        def pick(m, r):
            prod[m, r] = held.tile([P, T], F32, name=f"prod{m}_{r}")
            nc.vector.tensor_tensor(prod[m, r][:], y[m][:].indirect(pos_t[r][:]), gate_t[m, r][:], MULT)

        for m in range(BLOCKS):
            for r in range(2):
                pick(m, r)
        both = psum.tile([P, T], F32, name="both", tag="bank5")
        for r in range(2):
            nc.tensor.matmul(both[:], ident[:], prod[0, r][:], start=(r == 0), stop=(r == 1))
        nc.scalar.copy(total[0][:], both[:])
        nc.vector.tensor_add(total[1][:], prod[1, 0][:], prod[1, 1][:])
        for m in range(BLOCKS):
            nc.sync.dma_start(out=out[m * P : (m + 1) * P, :], in_=total[m][:])
